import numpy as np
import ml_dtypes


def mxq(x, axis, fmt="e4m3"):
    dtype, down = {"e4m3": (ml_dtypes.float8_e4m3fn, 7), "e5m2": (ml_dtypes.float8_e5m2, 14)}[fmt]
    v = np.moveaxis(np.asarray(x, np.float32).astype(ml_dtypes.bfloat16).astype(np.float64), axis, -1)
    blocks = v.reshape(v.shape[:-1] + (-1, 32))
    amax = np.abs(blocks).max(-1, keepdims=True)
    byte = np.maximum(np.where(amax > 0, np.frexp(amax)[1] - 1 + 127, 0) - down, 1)
    scale = np.exp2(byte - 127.0)
    codes = (blocks / scale).astype(np.float32).astype(dtype).astype(np.float64)
    return np.moveaxis((codes * scale).reshape(v.shape), -1, axis)


WIDE = False


def mx_kscale(k):
    if not WIDE:
        return np.ones(k)
    levels = np.array([10, -10, 5, -5, 0])
    if k % 512:
        return np.exp2(np.random.permutation(np.resize(levels, k // 32))).repeat(32)
    a = np.empty((k // 512, 16))
    for p in range(k // 512):
        a[p, :8] = np.random.permutation(np.resize(levels, 8))
        for g in range(8):
            far = levels[np.abs(levels - a[p, g]) >= 10]
            a[p, g + 8] = far[np.random.randint(len(far))]
    return np.exp2(a.ravel()).repeat(32)


def f64(x):
    return np.asarray(x).astype(np.float64)


def striped(idx):
    return np.tile(np.asarray(idx).reshape(-1, 16).T, (8, 1)).astype(np.uint16)


def unstriped(offs):
    return offs[:16].T.reshape(-1).astype(np.int64)


E2M1 = np.array([0.0, 0.5, 1.0, 1.5, 2.0, 3.0, 4.0, 6.0, -0.0, -0.5, -1.0, -1.5, -2.0, -3.0, -4.0, -6.0])


def pack_weight(w, fmt):
    k, n = w.shape
    w = f64(np.asarray(w, np.float32).astype(ml_dtypes.bfloat16)).reshape(k // 32, 32, n)
    amax = np.abs(w).max(1)
    if fmt == "e4m3":
        byte = np.frexp(amax)[1] - 1 + 127 - 7
    else:
        mant, ex = np.frexp(amax / 6.0)
        byte = np.where(mant > 0.5, ex, ex - 1) + 127
    byte = np.clip(np.where(amax > 0, byte, 1), 1, 254)
    scaled = (w * np.exp2(127.0 - byte)[:, None, :]).reshape(k, n).astype(np.float32)
    by_word = np.ascontiguousarray(scaled.reshape(k // 512, 128, 4, n).transpose(0, 1, 3, 2))
    if fmt == "e4m3":
        words = by_word.astype(ml_dtypes.float8_e4m3fn).view(np.uint8)
    else:
        c = by_word.astype(ml_dtypes.float4_e2m1fn).view(np.uint8) & 0xF
        words = (c[..., 0::2] | (c[..., 1::2] << 4)).reshape(k // 512, 128, 2 * n)
    return np.ascontiguousarray(words), np.ascontiguousarray(byte.astype(np.uint8).reshape(k // 512, 16, n))


def unpack_weight(words, scales, fmt):
    g, _, n = scales.shape
    words = np.ascontiguousarray(words).reshape(g, 128, n, -1)
    if fmt == "e4m3":
        vals = words.view(ml_dtypes.float8_e4m3fn).astype(np.float64)
    else:
        nib = np.empty((g, 128, n, 4), np.uint8)
        nib[..., 0::2] = words & 0xF
        nib[..., 1::2] = words >> 4
        vals = E2M1[nib]
    vals = vals * np.repeat(np.exp2(scales.astype(np.float64) - 127.0), 8, axis=1)[..., None]
    return vals.transpose(0, 1, 3, 2).reshape(g * 512, n)


D, T, I, G, U, Q = 512, 4096, 1024, 64, 512, 128


def setup_inputs():
    n = np.random.standard_normal
    idx = np.random.permutation(T)[:I]
    idx2 = np.random.permutation(U)[:G]
    fd = mx_kscale(D)
    keysp = pack_weight(n((D, T)) / fd[:, None], "e4m3")
    return {
        "query": (n((D, Q)) * 0.7 / np.sqrt(D) * fd[:, None]).astype(np.float32),
        "keys_words": keysp[0],
        "keys_scales": keysp[1],
        "old": (np.random.uniform(0.0, 16.0, (Q, U))).astype(np.float32),
        "fade": (np.random.uniform(0.5, 1.0, (1, U))).astype(np.float32),
        "offs": striped(idx),
        "offs2": striped(idx2),
    }


def reference(query, keys_words, keys_scales, old, fade, offs, offs2):
    idx = unstriped(offs)
    idx2 = unstriped(offs2)
    keysu = unpack_weight(keys_words, keys_scales, "e4m3")
    queryq = mxq(f64(query), 0, "e4m3")
    keysidxg = keysu[:, idx]
    a = queryq.T @ keysidxg
    p = np.exp(a - np.max(a, axis=1, keepdims=True))
    z = np.sum(p, axis=1, keepdims=True)
    r = p.reshape(Q, G, I // G).sum(axis=2) / z * 512.0
    rf = np.zeros((Q, U))
    rf[:, idx2] = r
    y = f64(old) * f64(fade) + rf
    return y

@@ -1,0 +1,153 @@
+from contextlib import ExitStack
+
+import concourse.mybir as mybir
+from concourse.masks import make_identity
+
+D, T, I, G, U, Q = 512, 4096, 1024, 64, 512, 128
+FLOPS = 2 * D * Q * I
+
+F32 = mybir.dt.float32
+BF16 = mybir.dt.bfloat16
+I32 = mybir.dt.int32
+U32 = mybir.dt.uint32
+U16 = mybir.dt.uint16
+U8 = mybir.dt.uint8
+FP8X4 = mybir.dt.float8_e4m3fn_x4
+ALU = mybir.AluOpType
+ACT = mybir.ActivationFunctionType
+AX = mybir.AxisListType
+
+P = 128
+HALF = I // 2
+PAGE = I // G
+MASS = 512.0
+B_FIRST = 320
+
+
+def tile_attend_pagemass_kernel(tc, query, keys_words, keys_scales, old, fade, offs, offs2, out):
+    nc = tc.nc
+    with ExitStack() as ctx:
+        sb = ctx.enter_context(tc.tile_pool(name="sb", bufs=1))
+        ps = ctx.enter_context(tc.psum_pool(name="ps", bufs=1))
+
+        slots = sb.tile([P, I // 16], U16, name="slots")
+        pages = sb.tile([P, G // 16], U16, name="pages")
+        q_raw = sb.tile([P, 4, Q], F32, name="q_raw")
+        fade_col = sb.tile([P, 4], F32, name="fade_col")
+        pool_words = sb.tile([P, T], I32, name="pool_words")
+        pool_scales = sb.tile([P, T], U8, name="pool_scales", tag="words0", align_bytes=64)
+        old_sb = sb.tile([P, U], F32, name="old_sb")
+
+        nc.sync.dma_start(slots[:], offs)
+        nc.sync.dma_start(
+            pool_scales[0:32, :].bitcast(I32),
+            keys_scales[0].bitcast(I32).unsqueeze(1).to_broadcast([16, 2, T // 4]),
+        )
+        nc.vector.memset(pool_scales[64:128, :].bitcast(I32), 0)
+        nc.vector.memset(pool_scales[32:64, :].bitcast(I32), 0)
+        nc.sync.dma_start(q_raw[:], query.rearrange("(p j) q -> p j q", j=4))
+        nc.sync.dma_start(fade_col[:], fade[0].rearrange("(p c) -> p c", c=4))
+        nc.sync.dma_start(pool_words[:], keys_words[0].rearrange("p n t -> p (n t)").bitcast(I32), max_dma_last_dim=4096)
+        nc.sync.dma_start(old_sb[:], old)
+        nc.sync.dma_start(pages[:], offs2)
+
+        placed = sb.tile([P, U], F32, name="placed")
+        ident = sb.tile([P, P], F32, name="ident")
+        k_scales = sb.tile([P, I], U8, name="k_scales", align_bytes=64)
+        nc.vector.memset(ident[:], 0.0)
+        nc.vector.memset(placed[:], 0.0)
+        nc.vector.memset(k_scales[:].bitcast(I32), 0)
+        make_identity(nc, ident[:], nomemset=True)
+
+        factor = sb.tile([P, G], F32, name="factor")
+        nc.scalar.activation(factor[:, G // 2 :], placed[:, : G // 2], ACT.Exp)
+
+        q_bf = sb.tile([P, Q, 4], BF16, name="q_bf", align_bytes=64)
+        q_codes = sb.tile([P, Q], U32, name="q_codes", align_bytes=64)
+        q_scales = sb.tile([P, Q], U8, name="q_scales", align_bytes=64)
+        nc.vector.tensor_copy(q_bf[:], q_raw[:].rearrange("p j q -> p q j"))
+        nc.vector.quantize_mx(
+            out=q_codes[:].bitcast(FP8X4), scales=q_scales[:], in_=q_bf[:].rearrange("p q j -> p (q j)")
+        )
+
+        picked_scales = sb.tile([P, I], U8, name="picked_scales")
+        nc.vector.tensor_copy(picked_scales[:], pool_scales[:].indirect(slots[:]))
+        for r in range(4):
+            nc.scalar.dma_start(k_scales[32 * r : 32 * r + 4, :].bitcast(I32), picked_scales[8 * r : 8 * r + 8 : 2, :].bitcast(I32))
+
+        fade_ps = ps.tile([P, 4, P], F32, name="fade_ps")
+        for c in range(4):
+            nc.tensor.transpose(fade_ps[:, c, :], fade_col[:, c : c + 1].to_broadcast([P, P]), ident[:])
+
+        scores = []
+        for h in range(2):
+            words = sb.tile([P, HALF], U32, name="words%d" % h, tag="words%d" % h, align_bytes=64)
+            lo = h * HALF // 16
+            nc.vector.tensor_copy(words[:], pool_words[:].bitcast(U32).indirect(slots[:, lo : lo + HALF // 16]))
+            bank = ps.tile([P, HALF], F32, name="bank%d" % h)
+            nc.tensor.matmul_mx(
+                out=bank[:],
+                lhsT=q_codes[:].bitcast(FP8X4),
+                lhsT_scale=q_scales[:],
+                rhs=words[:].bitcast(FP8X4),
+                rhs_scale=k_scales[:, h * HALF : (h + 1) * HALF],
+                start=True,
+                stop=True,
+            )
+            scores.append(bank)
+
+        neg_max_a = sb.tile([P, 1], F32, name="neg_max_a")
+        neg_max = sb.tile([P, 1], F32, name="neg_max")
+        nc.vector.tensor_reduce(neg_max_a[:], scores[0][:], AX.X, ALU.max, negate=True)
+
+        faded = sb.tile([P, U], F32, name="faded", tag="words0", align_bytes=64)
+        nc.vector.tensor_tensor(
+            faded[:].rearrange("q (p c) -> q p c", c=4),
+            old_sb[:].rearrange("q (p c) -> q p c", c=4),
+            fade_ps[:].rearrange("q c p -> q p c"),
+            ALU.mult,
+        )
+
+        neg_b = sb.tile([P, HALF], F32, name="neg_b")
+        nc.vector.tensor_scalar(
+            neg_b[:], scores[1][:], -1.0, neg_max_a[:], ALU.mult, ALU.min, accum_out=neg_max[:]
+        )
+
+        p_a = sb.tile([P, HALF], F32, name="p_a")
+        p_b1 = sb.tile([P, B_FIRST], F32, name="p_b1")
+        p_b2 = sb.tile([P, HALF - B_FIRST], F32, name="p_b2")
+        z_a = sb.tile([P, 1], F32, name="z_a")
+        z_b1 = sb.tile([P, 1], F32, name="z_b1")
+        z_b2 = sb.tile([P, 1], F32, name="z_b2")
+        nc.scalar.activation(p_a[:], scores[0][:], ACT.Exp, bias=neg_max_a[:], accum_out=z_a[:])
+        nc.scalar.activation(
+            factor[:, : G // 2], neg_max_a[:].to_broadcast([P, G // 2]), ACT.Exp, bias=neg_max[:], scale=-1.0
+        )
+        nc.scalar.activation(p_b1[:], neg_b[:, :B_FIRST], ACT.Exp, bias=neg_max[:], scale=-1.0, accum_out=z_b1[:])
+        nc.scalar.activation(p_b2[:], neg_b[:, B_FIRST:], ACT.Exp, bias=neg_max[:], scale=-1.0, accum_out=z_b2[:])
+
+        z_head = sb.tile([P, 1], F32, name="z_head")
+        z_tail = sb.tile([P, 1], F32, name="z_tail")
+        z_over = sb.tile([P, 1], F32, name="z_over")
+        nc.scalar.activation(z_head[:], z_a[:], ACT.Identity, bias=z_b1[:], scale=factor[:, 0:1])
+        nc.scalar.activation(z_tail[:], z_b2[:], ACT.Copy, scale=1.0 / MASS)
+        nc.scalar.activation(z_over[:], z_head[:], ACT.Identity, bias=z_tail[:], scale=1.0 / MASS)
+
+        sums = sb.tile([P, G], F32, name="sums")
+        first = 0
+        for part in (p_a, p_b1, p_b2):
+            count = part.shape[1] // PAGE
+            nc.vector.tensor_reduce(
+                sums[:, first : first + count], part[:].rearrange("q (g s) -> q g s", s=PAGE), AX.X, ALU.add
+            )
+            first = first + count
+
+        inv = sb.tile([P, 1], F32, name="inv")
+        nc.vector.reciprocal(inv[:], z_over[:])
+        nc.vector.tensor_tensor(placed[:].indirect(pages[:]), sums[:], factor[:], ALU.mult)
+
+        for h, queue in enumerate((nc.sync, nc.scalar)):
+            cols = slice(h * U // 2, (h + 1) * U // 2)
+            result = sb.tile([P, U // 2], F32, name="result%d" % h)
+            nc.vector.scalar_tensor_tensor(result[:], placed[:, cols], inv[:], faded[:, cols], ALU.mult, ALU.add)
+            queue.dma_start(out[:, cols], result[:])

@@ -19,9 +19,10 @@ AX = mybir.AxisListType
 
 P = 128
 HALF = I // 2
+CHUNKS = 4
+CHUNK = I // CHUNKS
 PAGE = I // G
 MASS = 512.0
-B_FIRST = 320
 
 
 def tile_attend_pagemass_kernel(tc, query, keys_words, keys_scales, old, fade, offs, offs2, out):
@@ -35,116 +36,114 @@ def tile_attend_pagemass_kernel(tc, query, keys_words, keys_scales, old, fade, o
         q_raw = sb.tile([P, 4, Q], F32, name="q_raw")
         fade_col = sb.tile([P, 4], F32, name="fade_col")
         pool_words = sb.tile([P, T], I32, name="pool_words")
-        pool_scales = sb.tile([P, T], U8, name="pool_scales", tag="words0", align_bytes=64)
-        old_sb = sb.tile([P, U], F32, name="old_sb")
+        pool_scales = sb.tile([P, T], U8, name="pool_scales", tag="scales_then_old")
 
         nc.sync.dma_start(slots[:], offs)
         nc.sync.dma_start(
             pool_scales[0:32, :].bitcast(I32),
             keys_scales[0].bitcast(I32).unsqueeze(1).to_broadcast([16, 2, T // 4]),
         )
+        nc.sync.dma_start(q_raw[:], query.rearrange("(p j) q -> p j q", j=4))
+        nc.sync.dma_start(pool_words[:], keys_words[0].rearrange("p n t -> p (n t)").bitcast(I32))
+        nc.sync.dma_start(fade_col[:], fade[0].rearrange("(p c) -> p c", c=4))
+        nc.sync.dma_start(pages[:], offs2)
         nc.vector.memset(pool_scales[64:128, :].bitcast(I32), 0)
         nc.vector.memset(pool_scales[32:64, :].bitcast(I32), 0)
-        nc.sync.dma_start(q_raw[:], query.rearrange("(p j) q -> p j q", j=4))
-        nc.sync.dma_start(fade_col[:], fade[0].rearrange("(p c) -> p c", c=4))
-        nc.sync.dma_start(pool_words[:], keys_words[0].rearrange("p n t -> p (n t)").bitcast(I32), max_dma_last_dim=4096)
-        nc.sync.dma_start(old_sb[:], old)
-        nc.sync.dma_start(pages[:], offs2)
 
-        placed = sb.tile([P, U], F32, name="placed")
         ident = sb.tile([P, P], F32, name="ident")
-        k_scales = sb.tile([P, I], U8, name="k_scales", align_bytes=64)
-        nc.vector.memset(ident[:], 0.0)
-        nc.vector.memset(placed[:], 0.0)
-        nc.vector.memset(k_scales[:].bitcast(I32), 0)
-        make_identity(nc, ident[:], nomemset=True)
+        make_identity(nc, ident[:])
 
-        factor = sb.tile([P, G], F32, name="factor")
-        nc.scalar.activation(factor[:, G // 2 :], placed[:, : G // 2], ACT.Exp)
+        picked_scales = sb.tile([P, I], U8, name="picked_scales")
+        k_scales = sb.tile([P, I], U8, name="k_scales", align_bytes=64)
+        nc.vector.tensor_copy(picked_scales[:], pool_scales[:].indirect(slots[:]))
+        nc.vector.memset(k_scales[:].bitcast(I32), 0)
+        for r in range(4):
+            nc.sync.dma_start(
+                k_scales[32 * r : 32 * r + 4, :].bitcast(I32), picked_scales[8 * r : 8 * r + 8 : 2, :].bitcast(I32)
+            )
+        old_sb = sb.tile([P, U], F32, name="old_sb", tag="scales_then_old")
+        nc.sync.dma_start(old_sb[:], old)
 
         q_bf = sb.tile([P, Q, 4], BF16, name="q_bf", align_bytes=64)
         q_codes = sb.tile([P, Q], U32, name="q_codes", align_bytes=64)
         q_scales = sb.tile([P, Q], U8, name="q_scales", align_bytes=64)
         nc.vector.tensor_copy(q_bf[:], q_raw[:].rearrange("p j q -> p q j"))
+        placed = sb.tile([P, U], F32, name="placed")
+        nc.vector.memset(placed[:], 0.0)
         nc.vector.quantize_mx(
             out=q_codes[:].bitcast(FP8X4), scales=q_scales[:], in_=q_bf[:].rearrange("p q j -> p (q j)")
         )
 
-        picked_scales = sb.tile([P, I], U8, name="picked_scales")
-        nc.vector.tensor_copy(picked_scales[:], pool_scales[:].indirect(slots[:]))
-        for r in range(4):
-            nc.scalar.dma_start(k_scales[32 * r : 32 * r + 4, :].bitcast(I32), picked_scales[8 * r : 8 * r + 8 : 2, :].bitcast(I32))
-
         fade_ps = ps.tile([P, 4, P], F32, name="fade_ps")
         for c in range(4):
             nc.tensor.transpose(fade_ps[:, c, :], fade_col[:, c : c + 1].to_broadcast([P, P]), ident[:])
+        fade_row = sb.tile([P, U], F32, name="fade_row")
+        nc.scalar.activation(
+            fade_row[:].rearrange("q (p c) -> q p c", c=4), fade_ps[:].rearrange("q c p -> q p c"), ACT.Copy
+        )
 
-        scores = []
+        banks = []
         for h in range(2):
             words = sb.tile([P, HALF], U32, name="words%d" % h, tag="words%d" % h, align_bytes=64)
             lo = h * HALF // 16
             nc.vector.tensor_copy(words[:], pool_words[:].bitcast(U32).indirect(slots[:, lo : lo + HALF // 16]))
-            bank = ps.tile([P, HALF], F32, name="bank%d" % h)
-            nc.tensor.matmul_mx(
-                out=bank[:],
-                lhsT=q_codes[:].bitcast(FP8X4),
-                lhsT_scale=q_scales[:],
-                rhs=words[:].bitcast(FP8X4),
-                rhs_scale=k_scales[:, h * HALF : (h + 1) * HALF],
-                start=True,
-                stop=True,
-            )
-            scores.append(bank)
-
-        neg_max_a = sb.tile([P, 1], F32, name="neg_max_a")
-        neg_max = sb.tile([P, 1], F32, name="neg_max")
-        nc.vector.tensor_reduce(neg_max_a[:], scores[0][:], AX.X, ALU.max, negate=True)
+            for first in range(0, HALF, CHUNK):
+                bank = ps.tile([P, CHUNK], F32, name="bank%d" % len(banks))
+                nc.tensor.matmul_mx(
+                    out=bank[:],
+                    lhsT=q_codes[:].bitcast(FP8X4),
+                    lhsT_scale=q_scales[:],
+                    rhs=words[:, first : first + CHUNK].bitcast(FP8X4),
+                    rhs_scale=k_scales[:, h * HALF + first : h * HALF + first + CHUNK],
+                    start=True,
+                    stop=True,
+                )
+                banks.append(bank)
 
         faded = sb.tile([P, U], F32, name="faded", tag="words0", align_bytes=64)
-        nc.vector.tensor_tensor(
-            faded[:].rearrange("q (p c) -> q p c", c=4),
-            old_sb[:].rearrange("q (p c) -> q p c", c=4),
-            fade_ps[:].rearrange("q c p -> q p c"),
-            ALU.mult,
-        )
+        nc.gpsimd.tensor_tensor(faded[:], old_sb[:], fade_row[:], ALU.mult)
 
-        neg_b = sb.tile([P, HALF], F32, name="neg_b")
-        nc.vector.tensor_scalar(
-            neg_b[:], scores[1][:], -1.0, neg_max_a[:], ALU.mult, ALU.min, accum_out=neg_max[:]
-        )
-
-        p_a = sb.tile([P, HALF], F32, name="p_a")
-        p_b1 = sb.tile([P, B_FIRST], F32, name="p_b1")
-        p_b2 = sb.tile([P, HALF - B_FIRST], F32, name="p_b2")
-        z_a = sb.tile([P, 1], F32, name="z_a")
-        z_b1 = sb.tile([P, 1], F32, name="z_b1")
-        z_b2 = sb.tile([P, 1], F32, name="z_b2")
-        nc.scalar.activation(p_a[:], scores[0][:], ACT.Exp, bias=neg_max_a[:], accum_out=z_a[:])
-        nc.scalar.activation(
-            factor[:, : G // 2], neg_max_a[:].to_broadcast([P, G // 2]), ACT.Exp, bias=neg_max[:], scale=-1.0
-        )
-        nc.scalar.activation(p_b1[:], neg_b[:, :B_FIRST], ACT.Exp, bias=neg_max[:], scale=-1.0, accum_out=z_b1[:])
-        nc.scalar.activation(p_b2[:], neg_b[:, B_FIRST:], ACT.Exp, bias=neg_max[:], scale=-1.0, accum_out=z_b2[:])
-
-        z_head = sb.tile([P, 1], F32, name="z_head")
-        z_tail = sb.tile([P, 1], F32, name="z_tail")
-        z_over = sb.tile([P, 1], F32, name="z_over")
-        nc.scalar.activation(z_head[:], z_a[:], ACT.Identity, bias=z_b1[:], scale=factor[:, 0:1])
-        nc.scalar.activation(z_tail[:], z_b2[:], ACT.Copy, scale=1.0 / MASS)
-        nc.scalar.activation(z_over[:], z_head[:], ACT.Identity, bias=z_tail[:], scale=1.0 / MASS)
-
-        sums = sb.tile([P, G], F32, name="sums")
-        first = 0
-        for part in (p_a, p_b1, p_b2):
-            count = part.shape[1] // PAGE
-            nc.vector.tensor_reduce(
-                sums[:, first : first + count], part[:].rearrange("q (g s) -> q g s", s=PAGE), AX.X, ALU.add
+        neg_maxes = sb.tile([P, CHUNKS], F32, name="neg_maxes")
+        chunk_sums = sb.tile([P, CHUNKS], F32, name="chunk_sums")
+        weights = sb.tile([P, I], F32, name="weights")
+        for c in range(CHUNKS):
+            nc.vector.tensor_reduce(neg_maxes[:, c : c + 1], banks[c][:], AX.X, ALU.max, negate=True)
+            nc.scalar.activation(
+                weights[:, c * CHUNK : (c + 1) * CHUNK],
+                banks[c][:],
+                ACT.Exp,
+                bias=neg_maxes[:, c : c + 1],
+                accum_out=chunk_sums[:, c : c + 1],
             )
-            first = first + count
 
+        page_sums = sb.tile([P, G], F32, name="page_sums")
+        neg_max = sb.tile([P, 1], F32, name="neg_max")
+        per = G // CHUNKS
+        for c in range(CHUNKS):
+            nc.vector.tensor_reduce(
+                page_sums[:, c * per : (c + 1) * per],
+                weights[:, c * CHUNK : (c + 1) * CHUNK].rearrange("q (g s) -> q g s", s=PAGE),
+                AX.X,
+                ALU.add,
+            )
+            if c == 0:
+                nc.vector.tensor_reduce(neg_max[:], neg_maxes[:], AX.X, ALU.min)
+
+        factor = sb.tile([P, CHUNKS, per], F32, name="factor")
+        nc.scalar.activation(
+            factor[:], neg_maxes[:].unsqueeze(2).to_broadcast([P, CHUNKS, per]), ACT.Exp, bias=neg_max[:], scale=-1.0
+        )
+
+        terms = sb.tile([P, CHUNKS], F32, name="terms")
+        z_over = sb.tile([P, 1], F32, name="z_over")
         inv = sb.tile([P, 1], F32, name="inv")
+        nc.vector.scalar_tensor_tensor(
+            terms[:], chunk_sums[:], 1.0 / MASS, factor[:, :, 0], ALU.mult, ALU.mult, accum_out=z_over[:]
+        )
+        nc.vector.tensor_tensor(
+            placed[:].indirect(pages[:]), page_sums[:], factor[:].rearrange("q c g -> q (c g)"), ALU.mult
+        )
         nc.vector.reciprocal(inv[:], z_over[:])
-        nc.vector.tensor_tensor(placed[:].indirect(pages[:]), sums[:], factor[:], ALU.mult)
 
         for h, queue in enumerate((nc.sync, nc.scalar)):
             cols = slice(h * U // 2, (h + 1) * U // 2)

@@ -18,11 +18,18 @@ ACT = mybir.ActivationFunctionType
 AX = mybir.AxisListType
 
 P = 128
+QUADRANT = 32
+PACK = 4
+BLOCKS = D // 32
+LIST_ROWS = 16
 HALF = I // 2
 CHUNKS = 4
 CHUNK = I // CHUNKS
 PAGE = I // G
+CHUNK_PAGES = CHUNK // PAGE
+FADE_RUN = U // P
 MASS = 512.0
+STORE_WIDTHS = (128, 192, 192)
 
 
 def tile_attend_pagemass_kernel(tc, query, keys_words, keys_scales, old, fade, offs, offs2, out):
@@ -31,70 +38,75 @@ def tile_attend_pagemass_kernel(tc, query, keys_words, keys_scales, old, fade, o
         sb = ctx.enter_context(tc.tile_pool(name="sb", bufs=1))
         ps = ctx.enter_context(tc.psum_pool(name="ps", bufs=1))
 
-        slots = sb.tile([P, I // 16], U16, name="slots")
-        pages = sb.tile([P, G // 16], U16, name="pages")
-        q_raw = sb.tile([P, 4, Q], F32, name="q_raw")
-        fade_col = sb.tile([P, 4], F32, name="fade_col")
+        token_list = sb.tile([P, I // LIST_ROWS], U16, name="token_list")
+        page_list = sb.tile([P, G // LIST_ROWS], U16, name="page_list")
+        q_raw = sb.tile([P, PACK, Q], F32, name="q_raw")
+        fade_runs = sb.tile([P, FADE_RUN], F32, name="fade_runs")
         pool_words = sb.tile([P, T], I32, name="pool_words")
         pool_scales = sb.tile([P, T], U8, name="pool_scales", tag="scales_then_old")
 
-        nc.sync.dma_start(slots[:], offs)
+        nc.sync.dma_start(token_list[:], offs)
         nc.sync.dma_start(
-            pool_scales[0:32, :].bitcast(I32),
-            keys_scales[0].bitcast(I32).unsqueeze(1).to_broadcast([16, 2, T // 4]),
+            pool_scales[0:QUADRANT, :].bitcast(I32),
+            keys_scales[0].bitcast(I32).unsqueeze(1).to_broadcast([BLOCKS, QUADRANT // BLOCKS, T // 4]),
         )
-        nc.sync.dma_start(q_raw[:], query.rearrange("(p j) q -> p j q", j=4))
+        nc.sync.dma_start(q_raw[:], query.rearrange("(p j) q -> p j q", j=PACK))
         nc.sync.dma_start(pool_words[:], keys_words[0].rearrange("p n t -> p (n t)").bitcast(I32))
-        nc.sync.dma_start(fade_col[:], fade[0].rearrange("(p c) -> p c", c=4))
-        nc.sync.dma_start(pages[:], offs2)
-        nc.vector.memset(pool_scales[64:128, :].bitcast(I32), 0)
-        nc.vector.memset(pool_scales[32:64, :].bitcast(I32), 0)
+        nc.sync.dma_start(fade_runs[:], fade[0].rearrange("(p c) -> p c", c=FADE_RUN))
+        nc.sync.dma_start(page_list[:], offs2)
+        nc.vector.memset(pool_scales[2 * QUADRANT : P, :].bitcast(I32), 0)
+        nc.vector.memset(pool_scales[QUADRANT : 2 * QUADRANT, :].bitcast(I32), 0)
 
         ident = sb.tile([P, P], F32, name="ident")
         make_identity(nc, ident[:])
 
         picked_scales = sb.tile([P, I], U8, name="picked_scales")
         k_scales = sb.tile([P, I], U8, name="k_scales", align_bytes=64)
-        nc.vector.tensor_copy(picked_scales[:], pool_scales[:].indirect(slots[:]))
+        nc.vector.tensor_copy(picked_scales[:], pool_scales[:].indirect(token_list[:]))
         nc.vector.memset(k_scales[:].bitcast(I32), 0)
-        for r in range(4):
+        for quad in range(P // QUADRANT):
             nc.sync.dma_start(
-                k_scales[32 * r : 32 * r + 4, :].bitcast(I32), picked_scales[8 * r : 8 * r + 8 : 2, :].bitcast(I32)
+                k_scales[QUADRANT * quad : QUADRANT * quad + 4, :].bitcast(I32),
+                picked_scales[8 * quad : 8 * quad + 8 : 2, :].bitcast(I32),
             )
         old_sb = sb.tile([P, U], F32, name="old_sb", tag="scales_then_old")
         nc.sync.dma_start(old_sb[:], old)
 
-        q_bf = sb.tile([P, Q, 4], BF16, name="q_bf", align_bytes=64)
-        q_codes = sb.tile([P, Q], U32, name="q_codes", align_bytes=64)
+        q_bf = sb.tile([P, Q, PACK], BF16, name="q_bf", align_bytes=64)
+        q_words = sb.tile([P, Q], U32, name="q_words", align_bytes=64)
         q_scales = sb.tile([P, Q], U8, name="q_scales", align_bytes=64)
         nc.vector.tensor_copy(q_bf[:], q_raw[:].rearrange("p j q -> p q j"))
         placed = sb.tile([P, U], F32, name="placed")
         nc.vector.memset(placed[:], 0.0)
         nc.vector.quantize_mx(
-            out=q_codes[:].bitcast(FP8X4), scales=q_scales[:], in_=q_bf[:].rearrange("p q j -> p (q j)")
+            out=q_words[:].bitcast(FP8X4), scales=q_scales[:], in_=q_bf[:].rearrange("p q j -> p (q j)")
         )
 
-        fade_ps = ps.tile([P, 4, P], F32, name="fade_ps")
-        for c in range(4):
-            nc.tensor.transpose(fade_ps[:, c, :], fade_col[:, c : c + 1].to_broadcast([P, P]), ident[:])
+        fade_ps = ps.tile([P, FADE_RUN, P], F32, name="fade_ps")
+        for c in range(FADE_RUN):
+            nc.tensor.transpose(fade_ps[:, c, :], fade_runs[:, c : c + 1].to_broadcast([P, P]), ident[:])
         fade_row = sb.tile([P, U], F32, name="fade_row")
         nc.scalar.activation(
-            fade_row[:].rearrange("q (p c) -> q p c", c=4), fade_ps[:].rearrange("q c p -> q p c"), ACT.Copy
+            fade_row[:].rearrange("q (p c) -> q p c", c=FADE_RUN),
+            fade_ps[:].rearrange("q c p -> q p c"),
+            ACT.Copy,
         )
 
         banks = []
-        for h in range(2):
+        for h in range(I // HALF):
             words = sb.tile([P, HALF], U32, name="words%d" % h, tag="words%d" % h, align_bytes=64)
-            lo = h * HALF // 16
-            nc.vector.tensor_copy(words[:], pool_words[:].bitcast(U32).indirect(slots[:, lo : lo + HALF // 16]))
-            for first in range(0, HALF, CHUNK):
+            column = h * HALF // LIST_ROWS
+            nc.vector.tensor_copy(
+                words[:], pool_words[:].bitcast(U32).indirect(token_list[:, column : column + HALF // LIST_ROWS])
+            )
+            for slot in range(0, HALF, CHUNK):
                 bank = ps.tile([P, CHUNK], F32, name="bank%d" % len(banks))
                 nc.tensor.matmul_mx(
                     out=bank[:],
-                    lhsT=q_codes[:].bitcast(FP8X4),
+                    lhsT=q_words[:].bitcast(FP8X4),
                     lhsT_scale=q_scales[:],
-                    rhs=words[:, first : first + CHUNK].bitcast(FP8X4),
-                    rhs_scale=k_scales[:, h * HALF + first : h * HALF + first + CHUNK],
+                    rhs=words[:, slot : slot + CHUNK].bitcast(FP8X4),
+                    rhs_scale=k_scales[:, h * HALF + slot : h * HALF + slot + CHUNK],
                     start=True,
                     stop=True,
                 )
@@ -118,10 +130,9 @@ def tile_attend_pagemass_kernel(tc, query, keys_words, keys_scales, old, fade, o
 
         page_sums = sb.tile([P, G], F32, name="page_sums")
         neg_max = sb.tile([P, 1], F32, name="neg_max")
-        per = G // CHUNKS
         for c in range(CHUNKS):
             nc.vector.tensor_reduce(
-                page_sums[:, c * per : (c + 1) * per],
+                page_sums[:, c * CHUNK_PAGES : (c + 1) * CHUNK_PAGES],
                 weights[:, c * CHUNK : (c + 1) * CHUNK].rearrange("q (g s) -> q g s", s=PAGE),
                 AX.X,
                 ALU.add,
@@ -129,9 +140,13 @@ def tile_attend_pagemass_kernel(tc, query, keys_words, keys_scales, old, fade, o
             if c == 0:
                 nc.vector.tensor_reduce(neg_max[:], neg_maxes[:], AX.X, ALU.min)
 
-        factor = sb.tile([P, CHUNKS, per], F32, name="factor")
+        factor = sb.tile([P, CHUNKS, CHUNK_PAGES], F32, name="factor")
         nc.scalar.activation(
-            factor[:], neg_maxes[:].unsqueeze(2).to_broadcast([P, CHUNKS, per]), ACT.Exp, bias=neg_max[:], scale=-1.0
+            factor[:],
+            neg_maxes[:].unsqueeze(2).to_broadcast([P, CHUNKS, CHUNK_PAGES]),
+            ACT.Exp,
+            bias=neg_max[:],
+            scale=-1.0,
         )
 
         terms = sb.tile([P, CHUNKS], F32, name="terms")
@@ -141,12 +156,14 @@ def tile_attend_pagemass_kernel(tc, query, keys_words, keys_scales, old, fade, o
             terms[:], chunk_sums[:], 1.0 / MASS, factor[:, :, 0], ALU.mult, ALU.mult, accum_out=z_over[:]
         )
         nc.vector.tensor_tensor(
-            placed[:].indirect(pages[:]), page_sums[:], factor[:].rearrange("q c g -> q (c g)"), ALU.mult
+            placed[:].indirect(page_list[:]), page_sums[:], factor[:].rearrange("q c g -> q (c g)"), ALU.mult
         )
         nc.vector.reciprocal(inv[:], z_over[:])
 
-        for h, queue in enumerate((nc.sync, nc.scalar)):
-            cols = slice(h * U // 2, (h + 1) * U // 2)
-            result = sb.tile([P, U // 2], F32, name="result%d" % h)
+        first = 0
+        for width in STORE_WIDTHS:
+            cols = slice(first, first + width)
+            result = sb.tile([P, width], F32, name="result%d" % first)
             nc.vector.scalar_tensor_tensor(result[:], placed[:, cols], inv[:], faded[:, cols], ALU.mult, ALU.add)
-            queue.dma_start(out[:, cols], result[:])
+            nc.sync.dma_start(out[:, cols], result[:])
+            first = first + width

from contextlib import ExitStack

import concourse.mybir as mybir
from concourse.masks import make_identity

D, T, I, G, U, Q = 512, 4096, 1024, 64, 512, 128
FLOPS = 2 * D * Q * I

F32 = mybir.dt.float32
BF16 = mybir.dt.bfloat16
I32 = mybir.dt.int32
U32 = mybir.dt.uint32
U16 = mybir.dt.uint16
U8 = mybir.dt.uint8
FP8X4 = mybir.dt.float8_e4m3fn_x4
ALU = mybir.AluOpType
ACT = mybir.ActivationFunctionType
AX = mybir.AxisListType

P = 128
QUADRANT = 32
PACK = 4
BLOCKS = D // 32
LIST_ROWS = 16
HALF = I // 2
CHUNKS = 4
CHUNK = I // CHUNKS
PAGE = I // G
CHUNK_PAGES = CHUNK // PAGE
FADE_RUN = U // P
MASS = 512.0
STORE_WIDTHS = (128, 192, 192)


def tile_attend_pagemass_kernel(tc, query, keys_words, keys_scales, old, fade, offs, offs2, out):
    nc = tc.nc
    with ExitStack() as ctx:
        sb = ctx.enter_context(tc.tile_pool(name="sb", bufs=1))
        ps = ctx.enter_context(tc.psum_pool(name="ps", bufs=1))

        token_list = sb.tile([P, I // LIST_ROWS], U16, name="token_list")
        page_list = sb.tile([P, G // LIST_ROWS], U16, name="page_list")
        q_raw = sb.tile([P, PACK, Q], F32, name="q_raw")
        fade_runs = sb.tile([P, FADE_RUN], F32, name="fade_runs")
        pool_words = sb.tile([P, T], I32, name="pool_words")
        pool_scales = sb.tile([P, T], U8, name="pool_scales", tag="scales_then_old")

        nc.sync.dma_start(token_list[:], offs)
        nc.sync.dma_start(
            pool_scales[0:QUADRANT, :].bitcast(I32),
            keys_scales[0].bitcast(I32).unsqueeze(1).to_broadcast([BLOCKS, QUADRANT // BLOCKS, T // 4]),
        )
        nc.sync.dma_start(q_raw[:], query.rearrange("(p j) q -> p j q", j=PACK))
        nc.sync.dma_start(pool_words[:], keys_words[0].rearrange("p n t -> p (n t)").bitcast(I32))
        nc.sync.dma_start(fade_runs[:], fade[0].rearrange("(p c) -> p c", c=FADE_RUN))
        nc.sync.dma_start(page_list[:], offs2)
        nc.vector.memset(pool_scales[2 * QUADRANT : P, :].bitcast(I32), 0)
        nc.vector.memset(pool_scales[QUADRANT : 2 * QUADRANT, :].bitcast(I32), 0)

        ident = sb.tile([P, P], F32, name="ident")
        make_identity(nc, ident[:])

        picked_scales = sb.tile([P, I], U8, name="picked_scales")
        k_scales = sb.tile([P, I], U8, name="k_scales", align_bytes=64)
        nc.vector.tensor_copy(picked_scales[:], pool_scales[:].indirect(token_list[:]))
        nc.vector.memset(k_scales[:].bitcast(I32), 0)
        for quad in range(P // QUADRANT):
            nc.sync.dma_start(
                k_scales[QUADRANT * quad : QUADRANT * quad + 4, :].bitcast(I32),
                picked_scales[8 * quad : 8 * quad + 8 : 2, :].bitcast(I32),
            )
        old_sb = sb.tile([P, U], F32, name="old_sb", tag="scales_then_old")
        nc.sync.dma_start(old_sb[:], old)

        q_bf = sb.tile([P, Q, PACK], BF16, name="q_bf", align_bytes=64)
        q_words = sb.tile([P, Q], U32, name="q_words", align_bytes=64)
        q_scales = sb.tile([P, Q], U8, name="q_scales", align_bytes=64)
        nc.vector.tensor_copy(q_bf[:], q_raw[:].rearrange("p j q -> p q j"))
        placed = sb.tile([P, U], F32, name="placed")
        nc.vector.memset(placed[:], 0.0)
        nc.vector.quantize_mx(
            out=q_words[:].bitcast(FP8X4), scales=q_scales[:], in_=q_bf[:].rearrange("p q j -> p (q j)")
        )

        fade_ps = ps.tile([P, FADE_RUN, P], F32, name="fade_ps")
        for c in range(FADE_RUN):
            nc.tensor.transpose(fade_ps[:, c, :], fade_runs[:, c : c + 1].to_broadcast([P, P]), ident[:])
        fade_row = sb.tile([P, U], F32, name="fade_row")
        nc.scalar.activation(
            fade_row[:].rearrange("q (p c) -> q p c", c=FADE_RUN),
            fade_ps[:].rearrange("q c p -> q p c"),
            ACT.Copy,
        )

        banks = []
        for h in range(I // HALF):
            words = sb.tile([P, HALF], U32, name="words%d" % h, tag="words%d" % h, align_bytes=64)
            column = h * HALF // LIST_ROWS
            nc.vector.tensor_copy(
                words[:], pool_words[:].bitcast(U32).indirect(token_list[:, column : column + HALF // LIST_ROWS])
            )
            for slot in range(0, HALF, CHUNK):
                bank = ps.tile([P, CHUNK], F32, name="bank%d" % len(banks))
                nc.tensor.matmul_mx(
                    out=bank[:],
                    lhsT=q_words[:].bitcast(FP8X4),
                    lhsT_scale=q_scales[:],
                    rhs=words[:, slot : slot + CHUNK].bitcast(FP8X4),
                    rhs_scale=k_scales[:, h * HALF + slot : h * HALF + slot + CHUNK],
                    start=True,
                    stop=True,
                )
                banks.append(bank)

        faded = sb.tile([P, U], F32, name="faded", tag="words0", align_bytes=64)
        nc.gpsimd.tensor_tensor(faded[:], old_sb[:], fade_row[:], ALU.mult)

        neg_maxes = sb.tile([P, CHUNKS], F32, name="neg_maxes")
        chunk_sums = sb.tile([P, CHUNKS], F32, name="chunk_sums")
        weights = sb.tile([P, I], F32, name="weights")
        for c in range(CHUNKS):
            nc.vector.tensor_reduce(neg_maxes[:, c : c + 1], banks[c][:], AX.X, ALU.max, negate=True)
            nc.scalar.activation(
                weights[:, c * CHUNK : (c + 1) * CHUNK],
                banks[c][:],
                ACT.Exp,
                bias=neg_maxes[:, c : c + 1],
                accum_out=chunk_sums[:, c : c + 1],
            )

        page_sums = sb.tile([P, G], F32, name="page_sums")
        neg_max = sb.tile([P, 1], F32, name="neg_max")
        for c in range(CHUNKS):
            nc.vector.tensor_reduce(
                page_sums[:, c * CHUNK_PAGES : (c + 1) * CHUNK_PAGES],
                weights[:, c * CHUNK : (c + 1) * CHUNK].rearrange("q (g s) -> q g s", s=PAGE),
                AX.X,
                ALU.add,
            )
            if c == 0:
                nc.vector.tensor_reduce(neg_max[:], neg_maxes[:], AX.X, ALU.min)

        factor = sb.tile([P, CHUNKS, CHUNK_PAGES], F32, name="factor")
        nc.scalar.activation(
            factor[:],
            neg_maxes[:].unsqueeze(2).to_broadcast([P, CHUNKS, CHUNK_PAGES]),
            ACT.Exp,
            bias=neg_max[:],
            scale=-1.0,
        )

        terms = sb.tile([P, CHUNKS], F32, name="terms")
        z_over = sb.tile([P, 1], F32, name="z_over")
        inv = sb.tile([P, 1], F32, name="inv")
        nc.vector.scalar_tensor_tensor(
            terms[:], chunk_sums[:], 1.0 / MASS, factor[:, :, 0], ALU.mult, ALU.mult, accum_out=z_over[:]
        )
        nc.vector.tensor_tensor(
            placed[:].indirect(page_list[:]), page_sums[:], factor[:].rearrange("q c g -> q (c g)"), ALU.mult
        )
        nc.vector.reciprocal(inv[:], z_over[:])

        first = 0
        for width in STORE_WIDTHS:
            cols = slice(first, first + width)
            result = sb.tile([P, width], F32, name="result%d" % first)
            nc.vector.scalar_tensor_tensor(result[:], placed[:, cols], inv[:], faded[:, cols], ALU.mult, ALU.add)
            nc.sync.dma_start(out[:, cols], result[:])
            first = first + width
